import numpy as np
import ml_dtypes


def mxq(x, axis, fmt="e4m3"):
    dtype, down = {"e4m3": (ml_dtypes.float8_e4m3fn, 7), "e5m2": (ml_dtypes.float8_e5m2, 14)}[fmt]
    v = np.moveaxis(np.asarray(x, np.float32).astype(ml_dtypes.bfloat16).astype(np.float64), axis, -1)
    blocks = v.reshape(v.shape[:-1] + (-1, 32))
    amax = np.abs(blocks).max(-1, keepdims=True)
    byte = np.maximum(np.where(amax > 0, np.frexp(amax)[1] - 1 + 127, 0) - down, 1)
    scale = np.exp2(byte - 127.0)
    codes = (blocks / scale).astype(np.float32).astype(dtype).astype(np.float64)
    return np.moveaxis((codes * scale).reshape(v.shape), -1, axis)


WIDE = False


def mx_kscale(k):
    if not WIDE:
        return np.ones(k)
    levels = np.array([10, -10, 5, -5, 0])
    if k % 512:
        return np.exp2(np.random.permutation(np.resize(levels, k // 32))).repeat(32)
    a = np.empty((k // 512, 16))
    for p in range(k // 512):
        a[p, :8] = np.random.permutation(np.resize(levels, 8))
        for g in range(8):
            far = levels[np.abs(levels - a[p, g]) >= 10]
            a[p, g + 8] = far[np.random.randint(len(far))]
    return np.exp2(a.ravel()).repeat(32)


def f64(x):
    return np.asarray(x).astype(np.float64)


def striped(idx):
    return np.tile(idx.reshape(-1, 16).T, (8, 1)).astype(np.uint16)


def unstriped(offs):
    return offs[:16].T.reshape(-1).astype(np.int64)


def pack_weight(w):
    k, n = w.shape
    w = f64(np.asarray(w, np.float32).astype(ml_dtypes.bfloat16)).reshape(k // 32, 32, n)
    amax = np.abs(w).max(1)
    byte = np.clip(np.where(amax > 0, np.frexp(amax)[1] - 1 + 127 - 7, 1), 1, 254)
    scaled = (w * np.exp2(127.0 - byte)[:, None, :]).reshape(k, n).astype(np.float32)
    words = np.ascontiguousarray(scaled.reshape(k // 512, 128, 4, n).transpose(0, 1, 3, 2)).astype(ml_dtypes.float8_e4m3fn).view(np.uint8)
    return words, np.ascontiguousarray(byte.astype(np.uint8).reshape(k // 512, 16, n))


def unpack_weight(words, scales):
    g, p, n, _ = words.shape
    vals = np.ascontiguousarray(words).view(ml_dtypes.float8_e4m3fn).astype(np.float64) * np.repeat(np.exp2(scales.astype(np.float64) - 127.0), 8, axis=1)[..., None]
    return vals.transpose(0, 1, 3, 2).reshape(g * 512, n)


def relu(v):
    return np.maximum(v, 0.0)


K, T, S, N, H = 1024, 2048, 1024, 128, 512


def setup_inputs():
    n = np.random.standard_normal
    s = mx_kscale(K)[:, None]
    c = mx_kscale(S)
    packed_xT = pack_weight(n((K, T)) * s)
    return {
        "x_words": packed_xT[0],
        "x_scales": packed_xT[1],
        "py": (n((K, H)) / np.sqrt(K) / s).astype(np.float32),
        "pzz1": (n((K, N)) / np.sqrt(K) / s).astype(np.float32),
        "wa": (np.random.uniform(0.4, 1.0, (S, 1)) * c[:, None] / np.sqrt(S)).astype(np.float32),
        "wb": (np.random.uniform(0.6, 1.4, (S, 1)) / c[:, None]).astype(np.float32),
        "mom": (n((H, N))).astype(np.float32),
        "offs": striped(np.random.permutation(T)[:S]),
    }


def reference(x_words, x_scales, py, pzz1, wa, wb, mom, offs):
    xq = unpack_weight(x_words, x_scales)[:, unstriped(offs)]
    pyq = mxq(f64(py), 0, "e4m3")
    y = xq.T @ pyq
    ya = np.tanh(y)
    ka = f64(wa) * ya
    pzz1q = mxq(f64(pzz1), 0, "e4m3")
    zz1 = xq.T @ pzz1q
    zb = zz1 - relu(0.5 * zz1)
    kv = f64(wb) * zb
    gr = mxq(ka, 0, "e4m3").T @ mxq(kv, 0, "e4m3")
    mnew = 0.7 * f64(mom) + gr
    m2 = (mnew) ** 2
    rowm = m2.mean(axis=1, keepdims=True)
    return mnew / np.sqrt(rowm + 0.1)

@@ -1,0 +1,248 @@
+from contextlib import ExitStack
+
+import concourse.mybir as mybir
+from concourse.masks import make_identity
+
+K, T, S, N, H = 1024, 2048, 1024, 128, 512
+FLOPS = 2 * K * S * (H + N) + 2 * S * H * N
+
+F32 = mybir.dt.float32
+BF16 = mybir.dt.bfloat16
+I32 = mybir.dt.int32
+U32 = mybir.dt.uint32
+U16 = mybir.dt.uint16
+U8 = mybir.dt.uint8
+FP8X4 = mybir.dt.float8_e4m3fn_x4
+ACT = mybir.ActivationFunctionType
+ALU = mybir.AluOpType
+
+P = 128
+PACK = 4
+K_PASS = P * PACK
+K_PASSES = K // K_PASS
+S_PASSES = S // K_PASS
+RUN = 8
+HALF = 256
+COLS = 128
+CHUNKS = H // COLS
+
+
+def tile_picked_yshamp_leak_p_kernel(
+    tc, x_words, x_scales, py, pzz1, wa, wb, mom, offs, out
+):
+    nc = tc.nc
+    with ExitStack() as ctx:
+        keep = ctx.enter_context(tc.tile_pool(name="keep", bufs=1))
+        ring = ctx.enter_context(tc.tile_pool(name="ring", bufs=4))
+        acc_pool = ctx.enter_context(tc.psum_pool(name="acc", bufs=5))
+        one_pool = ctx.enter_context(tc.psum_pool(name="one", bufs=1))
+
+        offsets = keep.tile([P, S // 16], U16, name="offsets")
+        nc.sync.dma_start(offsets[:], offs)
+        scale_table = keep.tile([P, T], U8, name="scale_table", align_bytes=64)
+        nc.vector.memset(scale_table[:].bitcast(I32), 0)
+        factor_rows = keep.tile([P, S_PASSES * P], F32, name="factor_rows")
+        nc.gpsimd.memset(factor_rows[:], 0.0)
+        identity = keep.tile([P, P], F32, name="identity")
+        make_identity(nc, identity[:])
+
+        word_table = {}
+        py_raw = {}
+
+        def load_words(o):
+            word_table[o] = keep.tile([P, T], U32, name="word_table%d" % o, align_bytes=64)
+            nc.sync.dma_start(
+                out=word_table[o][:].bitcast(I32),
+                in_=x_words[o].rearrange("p n t -> p (n t)").bitcast(I32),
+            )
+
+        def load_py(h, o):
+            py_raw[h, o] = keep.tile([P, PACK, HALF], F32, name="py_raw%d%d" % (h, o))
+            rows = py[o * K_PASS : (o + 1) * K_PASS, h * HALF : (h + 1) * HALF]
+            nc.sync.dma_start(out=py_raw[h, o][:], in_=rows.rearrange("(p j) n -> p j n", j=PACK))
+
+        def load_scales():
+            for q in range(4):
+                nc.sync.dma_start(
+                    out=scale_table[32 * q : 32 * q + 4 * K_PASSES, :].bitcast(I32),
+                    in_=x_scales[:, 4 * q : 4 * q + 4, :].bitcast(I32),
+                )
+
+        pz_raw = keep.tile([P, K_PASSES, PACK, N], F32, name="pz_raw")
+        mom_sb = keep.tile([P, CHUNKS, N], F32, name="mom_sb")
+        load_words(0)
+        load_scales()
+        nc.sync.dma_start(out=pz_raw[:], in_=pzz1.rearrange("(o p j) n -> p o j n", o=K_PASSES, j=PACK))
+        load_words(1)
+        load_py(0, 0)
+        load_py(0, 1)
+        load_py(1, 0)
+        load_py(1, 1)
+        nc.sync.dma_start(out=mom_sb[:], in_=mom.rearrange("(c p) m -> p c m", p=P))
+        for a, w in enumerate((wa, wb)):
+            nc.scalar.dma_start(
+                out=factor_rows[PACK * a : PACK * (a + 1), :].rearrange("j (g r) -> j g r", r=RUN),
+                in_=w.rearrange("(g j r) o -> j g (r o)", j=PACK, r=RUN),
+            )
+
+        def gather(dtype, table, b, name):
+            picked = keep.tile([P, K_PASS], dtype, name=name, align_bytes=64)
+            cols = K_PASS // 16
+            nc.vector.tensor_copy(
+                out=picked[:].rearrange("p (j g r) -> p g j r", j=PACK, r=RUN),
+                in_=table.indirect(offsets[:, b * cols : (b + 1) * cols]),
+            )
+            return picked
+
+        def interleave(copy, dst, src):
+            copy(
+                out=dst.rearrange("p (c i) t -> p c t i", i=4),
+                in_=src.rearrange("p t (c i) -> p c t i", i=4),
+            )
+
+        def quantise(values, width, name):
+            codes = keep.tile([P, width], U32, name=name + "_codes", align_bytes=64)
+            scales = keep.tile([P, width], U8, name=name + "_scales", align_bytes=64)
+            nc.vector.quantize_mx(out=codes[:].bitcast(FP8X4), scales=scales[:], in_=values)
+            return codes, scales
+
+        x_code = {}
+        x_scale = {}
+
+        def pick_words(o, b):
+            x_code[o, b] = gather(U32, word_table[o][:], b, "x_code%d%d" % (o, b))
+
+        def pick_scales(b):
+            x_scale[b] = gather(U8, scale_table[:], b, "x_scale%d" % b)
+
+        def prepare_pz():
+            pz_bf = keep.tile([P, K_PASSES, N, PACK], BF16, name="pz_bf", align_bytes=64)
+            for o in range(K_PASSES):
+                interleave(nc.scalar.copy, pz_bf[:, o], pz_raw[:, o])
+            return quantise(pz_bf[:].rearrange("p o n t -> p (o n t)"), K_PASSES * N, "pz")
+
+        turned = one_pool.tile([P, S_PASSES, P], F32, name="turned")
+        for b in range(S_PASSES):
+            nc.tensor.transpose(turned[:, b, :], factor_rows[:, b * P : (b + 1) * P], identity[:])
+        factors = keep.tile([P, S_PASSES, 2 * PACK], F32, name="factors")
+        nc.scalar.activation(out=factors[:, :, 0:PACK], in_=turned[:, :, 0:PACK], func=ACT.Copy)
+        nc.scalar.activation(out=factors[:, :, PACK:], in_=turned[:, :, PACK : 2 * PACK], func=ACT.Copy, scale=-0.25)
+
+        def project(b, weights):
+            acc = acc_pool.tile([P, PACK, COLS], F32, name="acc")
+            for j in range(PACK):
+                cols = slice(j * P, (j + 1) * P)
+                for o in range(K_PASSES):
+                    codes, scales = weights[o]
+                    nc.tensor.matmul_mx(
+                        out=acc[:, j, :],
+                        lhsT=x_code[o, b][:, cols].bitcast(FP8X4),
+                        lhsT_scale=x_scale[b][4 * o :, cols],
+                        rhs=codes.bitcast(FP8X4),
+                        rhs_scale=scales,
+                        start=(o == 0),
+                        stop=(o == K_PASSES - 1),
+                    )
+            return acc
+
+        py_q = {}
+
+        def prepare_py(h, o, copy):
+            py_bf = ring.tile([P, HALF, PACK], BF16, name="py_bf", align_bytes=64)
+            interleave(copy, py_bf[:], py_raw[h, o][:])
+            py_q[h, o] = quantise(py_bf[:].rearrange("p n t -> p (n t)"), HALF, "py%d%d" % (h, o))
+
+        def second_factor(b):
+            z = project(b, [(pz_q[0][:, o * N : (o + 1) * N], pz_q[1][:, o * N : (o + 1) * N]) for o in range(K_PASSES)])
+            sign = ring.tile([P, COLS, PACK], F32, name="sign")
+            nc.scalar.activation(out=sign[:], in_=z[:].rearrange("p j n -> p n j"), func=ACT.Sign)
+            scaled = ring.tile([P, PACK, COLS], F32, name="scaled")
+            for j in range(PACK):
+                nc.scalar.activation(
+                    out=scaled[:, j, :], in_=z[:, j, :], func=ACT.Copy, scale=factors[:, b, PACK + j : PACK + j + 1]
+                )
+            rounded = ring.tile([P, COLS, PACK], BF16, name="kv_rounded", align_bytes=64)
+            nc.vector.scalar_tensor_tensor(
+                out=rounded[:], in0=sign[:], scalar=-3.0, in1=scaled[:].rearrange("p j n -> p n j"),
+                op0=ALU.add, op1=ALU.mult,
+            )
+            return quantise(rounded[:].rearrange("p n j -> p (n j)"), COLS, "kv%d" % b)
+
+        def first_factor(c):
+            h, lo = divmod(c * COLS, HALF)
+            cols = slice(lo, lo + COLS)
+            bent = ring.tile([P, S_PASSES, COLS, PACK], F32, name="bent")
+            for b in range(S_PASSES):
+                y = project(b, [(py_q[h, o][0][:, cols], py_q[h, o][1][:, cols]) for o in range(K_PASSES)])
+                nc.scalar.activation(out=bent[:, b], in_=y[:].rearrange("p j n -> p n j"), func=ACT.Tanh)
+            rounded = ring.tile([P, S_PASSES, COLS, PACK], BF16, name="ka_rounded", align_bytes=64)
+            factor = factors[:, :, 0:PACK].unsqueeze(2).to_broadcast([P, S_PASSES, COLS, PACK])
+            nc.vector.tensor_tensor(out=rounded[:], in0=bent[:], in1=factor, op=ALU.mult)
+            return quantise(rounded[:].rearrange("p b n j -> p (b n j)"), S_PASSES * COLS, "ka%d" % c)
+
+        moment = keep.tile([P, CHUNKS, N], F32, name="moment")
+        squares = [keep.tile([P, N], F32, name="squares%d" % e) for e in range(2)]
+        sums = keep.tile([P, CHUNKS], F32, name="sums")
+
+        def update(c, ka):
+            outer = one_pool.tile([P, N], F32, name="outer%d" % (c % 2))
+            for b in range(S_PASSES):
+                cols = slice(b * COLS, (b + 1) * COLS)
+                nc.tensor.matmul_mx(
+                    out=outer[:],
+                    lhsT=ka[0][:, cols].bitcast(FP8X4),
+                    lhsT_scale=ka[1][:, cols],
+                    rhs=kv[b][0][:].bitcast(FP8X4),
+                    rhs_scale=kv[b][1][:],
+                    start=(b == 0),
+                    stop=(b == S_PASSES - 1),
+                )
+            nc.vector.scalar_tensor_tensor(
+                out=moment[:, c, :], in0=mom_sb[:, c, :], scalar=0.7, in1=outer[:], op0=ALU.mult, op1=ALU.add
+            )
+            if c < 1:
+                nc.scalar.activation(
+                    out=squares[0][:], in_=moment[:, c, :], func=ACT.Square, scale=N**-0.5, accum_out=sums[:, c : c + 1]
+                )
+            else:
+                nc.vector.scalar_tensor_tensor(
+                    out=squares[1][:], in0=moment[:, c, :], scalar=1.0 / N, in1=moment[:, c, :],
+                    op0=ALU.mult, op1=ALU.mult, accum_out=sums[:, c : c + 1],
+                )
+
+        pick_words(0, 0)
+        pick_scales(0)
+        pick_words(0, 1)
+        pz_q = prepare_pz()
+        pick_words(1, 0)
+        pick_scales(1)
+        pick_words(1, 1)
+        prepare_py(0, 0, nc.scalar.copy)
+        kv = [second_factor(0)]
+        prepare_py(0, 1, nc.scalar.copy)
+        kv.append(second_factor(1))
+        ka0 = first_factor(0)
+        prepare_py(1, 0, nc.scalar.copy)
+        prepare_py(1, 1, nc.vector.tensor_copy)
+        ka1 = first_factor(1)
+        update(0, ka0)
+        ka2 = first_factor(2)
+        update(1, ka1)
+        ka3 = first_factor(3)
+        update(2, ka2)
+        update(3, ka3)
+
+        inv_rms = keep.tile([P, CHUNKS], F32, name="inv_rms")
+        nc.scalar.activation(out=inv_rms[:], in_=sums[:], func=ACT.Abs_reciprocal_sqrt, bias=0.1)
+        out_rows = out.rearrange("(c p) m -> p c m", p=P)
+        for half, queue in enumerate((nc.sync, nc.scalar)):
+            result = keep.tile([P, 2, N], F32, name="result%d" % half)
+            for e in range(2):
+                c = 2 * half + e
+                if half == 0:
+                    nc.vector.tensor_scalar(
+                        out=result[:, e, :], in0=moment[:, c, :], scalar1=inv_rms[:, c : c + 1], scalar2=None, op0=ALU.mult
+                    )
+                else:
+                    nc.scalar.activation(out=result[:, e, :], in_=moment[:, c, :], func=ACT.Copy, scale=inv_rms[:, c : c + 1])
+            queue.dma_start(out=out_rows[:, 2 * half : 2 * half + 2, :], in_=result[:])

@@ -1,7 +1,6 @@
 from contextlib import ExitStack
 
 import concourse.mybir as mybir
-from concourse.masks import make_identity
 
 K, T, S, N, H = 1024, 2048, 1024, 128, 512
 FLOPS = 2 * K * S * (H + N) + 2 * S * H * N
@@ -42,22 +41,29 @@ def tile_picked_yshamp_leak_p_kernel(
         scale_table = keep.tile([P, T], U8, name="scale_table", align_bytes=64)
         nc.vector.memset(scale_table[:].bitcast(I32), 0)
         factor_rows = keep.tile([P, S_PASSES * P], F32, name="factor_rows")
-        nc.gpsimd.memset(factor_rows[:], 0.0)
+        nc.vector.memset(factor_rows[:], 0.0)
         identity = keep.tile([P, P], F32, name="identity")
-        make_identity(nc, identity[:])
+        with tc.tile_pool(name="scratch", bufs=1) as scratch:
+            zeros = scratch.tile([P, P], F32, name="zeros")
+            nc.gpsimd.memset(zeros[:], 0.0)
+            nc.gpsimd.affine_select(
+                out=identity[:], in_=zeros[:], pattern=[[-1, P]], compare_op=ALU.not_equal, fill=1.0,
+                base=0, channel_multiplier=1,
+            )
+        late = ctx.enter_context(tc.tile_pool(name="late", bufs=1))
 
         word_table = {}
         py_raw = {}
 
         def load_words(o):
-            word_table[o] = keep.tile([P, T], U32, name="word_table%d" % o, align_bytes=64)
+            word_table[o] = late.tile([P, T], U32, name="word_table%d" % o, align_bytes=64)
             nc.sync.dma_start(
                 out=word_table[o][:].bitcast(I32),
                 in_=x_words[o].rearrange("p n t -> p (n t)").bitcast(I32),
             )
 
         def load_py(h, o):
-            py_raw[h, o] = keep.tile([P, PACK, HALF], F32, name="py_raw%d%d" % (h, o))
+            py_raw[h, o] = late.tile([P, PACK, HALF], F32, name="py_raw%d%d" % (h, o))
             rows = py[o * K_PASS : (o + 1) * K_PASS, h * HALF : (h + 1) * HALF]
             nc.sync.dma_start(out=py_raw[h, o][:], in_=rows.rearrange("(p j) n -> p j n", j=PACK))
 
@@ -68,22 +74,25 @@ def tile_picked_yshamp_leak_p_kernel(
                     in_=x_scales[:, 4 * q : 4 * q + 4, :].bitcast(I32),
                 )
 
+        def load_factors():
+            for a, w in enumerate((wa, wb)):
+                nc.sync.dma_start(
+                    out=factor_rows[PACK * a : PACK * (a + 1), :].rearrange("j (g r) -> j g r", r=RUN),
+                    in_=w.rearrange("(g j r) o -> j g (r o)", j=PACK, r=RUN),
+                )
+
         pz_raw = keep.tile([P, K_PASSES, PACK, N], F32, name="pz_raw")
-        mom_sb = keep.tile([P, CHUNKS, N], F32, name="mom_sb")
-        load_words(0)
-        load_scales()
+        mom_sb = late.tile([P, CHUNKS, N], F32, name="mom_sb")
         nc.sync.dma_start(out=pz_raw[:], in_=pzz1.rearrange("(o p j) n -> p o j n", o=K_PASSES, j=PACK))
-        load_words(1)
+        load_scales()
+        load_factors()
+        load_words(0)
         load_py(0, 0)
+        load_words(1)
         load_py(0, 1)
         load_py(1, 0)
         load_py(1, 1)
         nc.sync.dma_start(out=mom_sb[:], in_=mom.rearrange("(c p) m -> p c m", p=P))
-        for a, w in enumerate((wa, wb)):
-            nc.scalar.dma_start(
-                out=factor_rows[PACK * a : PACK * (a + 1), :].rearrange("j (g r) -> j g r", r=RUN),
-                in_=w.rearrange("(g j r) o -> j g (r o)", j=PACK, r=RUN),
-            )
 
         def gather(dtype, table, b, name):
             picked = keep.tile([P, K_PASS], dtype, name=name, align_bytes=64)
@@ -121,15 +130,18 @@ def tile_picked_yshamp_leak_p_kernel(
                 interleave(nc.scalar.copy, pz_bf[:, o], pz_raw[:, o])
             return quantise(pz_bf[:].rearrange("p o n t -> p (o n t)"), K_PASSES * N, "pz")
 
-        turned = one_pool.tile([P, S_PASSES, P], F32, name="turned")
+        turned = one_pool.tile([P, S_PASSES, P], F32, name="turned", tag="shared_bank")
         for b in range(S_PASSES):
             nc.tensor.transpose(turned[:, b, :], factor_rows[:, b * P : (b + 1) * P], identity[:])
         factors = keep.tile([P, S_PASSES, 2 * PACK], F32, name="factors")
         nc.scalar.activation(out=factors[:, :, 0:PACK], in_=turned[:, :, 0:PACK], func=ACT.Copy)
         nc.scalar.activation(out=factors[:, :, PACK:], in_=turned[:, :, PACK : 2 * PACK], func=ACT.Copy, scale=-0.25)
 
-        def project(b, weights):
-            acc = acc_pool.tile([P, PACK, COLS], F32, name="acc")
+        def project(b, weights, last=False):
+            if last:
+                acc = one_pool.tile([P, PACK, COLS], F32, name="last_acc", tag="shared_bank")
+            else:
+                acc = acc_pool.tile([P, PACK, COLS], F32, name="acc")
             for j in range(PACK):
                 cols = slice(j * P, (j + 1) * P)
                 for o in range(K_PASSES):
@@ -173,19 +185,23 @@ def tile_picked_yshamp_leak_p_kernel(
             cols = slice(lo, lo + COLS)
             bent = ring.tile([P, S_PASSES, COLS, PACK], F32, name="bent")
             for b in range(S_PASSES):
-                y = project(b, [(py_q[h, o][0][:, cols], py_q[h, o][1][:, cols]) for o in range(K_PASSES)])
+                weights = [(py_q[h, o][0][:, cols], py_q[h, o][1][:, cols]) for o in range(K_PASSES)]
+                y = project(b, weights, last=(c == CHUNKS - 1 and b == S_PASSES - 1))
                 nc.scalar.activation(out=bent[:, b], in_=y[:].rearrange("p j n -> p n j"), func=ACT.Tanh)
+            return bent
+
+        def weigh_first(c, bent):
             rounded = ring.tile([P, S_PASSES, COLS, PACK], BF16, name="ka_rounded", align_bytes=64)
             factor = factors[:, :, 0:PACK].unsqueeze(2).to_broadcast([P, S_PASSES, COLS, PACK])
             nc.vector.tensor_tensor(out=rounded[:], in0=bent[:], in1=factor, op=ALU.mult)
             return quantise(rounded[:].rearrange("p b n j -> p (b n j)"), S_PASSES * COLS, "ka%d" % c)
 
         moment = keep.tile([P, CHUNKS, N], F32, name="moment")
-        squares = [keep.tile([P, N], F32, name="squares%d" % e) for e in range(2)]
-        sums = keep.tile([P, CHUNKS], F32, name="sums")
+        first_sum = keep.tile([P, 1], F32, name="first_sum", tag="sum_then_squares")
+        later_sums = keep.tile([P, CHUNKS - 1], F32, name="later_sums")
 
         def update(c, ka):
-            outer = one_pool.tile([P, N], F32, name="outer%d" % (c % 2))
+            outer = one_pool.tile([P, N], F32, name="outer%d" % c, tag="outer%d" % (c % 2) if c else "shared_bank")
             for b in range(S_PASSES):
                 cols = slice(b * COLS, (b + 1) * COLS)
                 nc.tensor.matmul_mx(
@@ -200,49 +216,58 @@ def tile_picked_yshamp_leak_p_kernel(
             nc.vector.scalar_tensor_tensor(
                 out=moment[:, c, :], in0=mom_sb[:, c, :], scalar=0.7, in1=outer[:], op0=ALU.mult, op1=ALU.add
             )
-            if c < 1:
-                nc.scalar.activation(
-                    out=squares[0][:], in_=moment[:, c, :], func=ACT.Square, scale=N**-0.5, accum_out=sums[:, c : c + 1]
+            if c == 0:
+                squares = keep.tile([P, N], F32, name="first_squares")
+                nc.vector.scalar_tensor_tensor(
+                    out=squares[:], in0=moment[:, c, :], scalar=1.0 / N, in1=moment[:, c, :],
+                    op0=ALU.mult, op1=ALU.mult, accum_out=first_sum[:],
                 )
             else:
-                nc.vector.scalar_tensor_tensor(
-                    out=squares[1][:], in0=moment[:, c, :], scalar=1.0 / N, in1=moment[:, c, :],
-                    op0=ALU.mult, op1=ALU.mult, accum_out=sums[:, c : c + 1],
+                squares = keep.tile([P, N], F32, name="squares%d" % c, tag="sum_then_squares")
+                nc.scalar.activation(
+                    out=squares[:], in_=moment[:, c, :], func=ACT.Square, scale=N**-0.5,
+                    accum_out=later_sums[:, c - 1 : c],
                 )
 
-        pick_words(0, 0)
-        pick_scales(0)
-        pick_words(0, 1)
-        pz_q = prepare_pz()
-        pick_words(1, 0)
-        pick_scales(1)
-        pick_words(1, 1)
-        prepare_py(0, 0, nc.scalar.copy)
-        kv = [second_factor(0)]
-        prepare_py(0, 1, nc.scalar.copy)
-        kv.append(second_factor(1))
-        ka0 = first_factor(0)
-        prepare_py(1, 0, nc.scalar.copy)
-        prepare_py(1, 1, nc.vector.tensor_copy)
-        ka1 = first_factor(1)
-        update(0, ka0)
-        ka2 = first_factor(2)
-        update(1, ka1)
-        ka3 = first_factor(3)
-        update(2, ka2)
-        update(3, ka3)
-
-        inv_rms = keep.tile([P, CHUNKS], F32, name="inv_rms")
-        nc.scalar.activation(out=inv_rms[:], in_=sums[:], func=ACT.Abs_reciprocal_sqrt, bias=0.1)
         out_rows = out.rearrange("(c p) m -> p c m", p=P)
-        for half, queue in enumerate((nc.sync, nc.scalar)):
-            result = keep.tile([P, 2, N], F32, name="result%d" % half)
-            for e in range(2):
-                c = 2 * half + e
-                if half == 0:
-                    nc.vector.tensor_scalar(
-                        out=result[:, e, :], in0=moment[:, c, :], scalar1=inv_rms[:, c : c + 1], scalar2=None, op0=ALU.mult
-                    )
-                else:
-                    nc.scalar.activation(out=result[:, e, :], in_=moment[:, c, :], func=ACT.Copy, scale=inv_rms[:, c : c + 1])
-            queue.dma_start(out=out_rows[:, 2 * half : 2 * half + 2, :], in_=result[:])
+
+        def finish(first, count):
+            cols = slice(first, first + count)
+            means = later_sums[:, first - 1 : first - 1 + count] if first else first_sum[:]
+            inv_rms = keep.tile([P, count], F32, name="inv_rms%d" % first)
+            nc.scalar.activation(out=inv_rms[:], in_=means, func=ACT.Abs_reciprocal_sqrt, bias=0.1)
+            result = keep.tile([P, count, N], F32, name="result%d" % first)
+            for e in range(count):
+                nc.scalar.activation(
+                    out=result[:, e, :], in_=moment[:, first + e, :], func=ACT.Copy, scale=inv_rms[:, e : e + 1]
+                )
+            nc.sync.dma_start(out=out_rows[:, cols, :], in_=result[:])
+
+        pick_scales(0)
+        pick_scales(1)
+        pz_q = prepare_pz()
+        pick_words(0, 0)
+        pick_words(0, 1)
+        prepare_py(0, 0, nc.scalar.copy)
+        pick_words(1, 0)
+        pick_words(1, 1)
+        prepare_py(0, 1, nc.scalar.copy)
+        prepare_py(1, 0, nc.vector.tensor_copy)
+        kv = [second_factor(0)]
+        prepare_py(1, 1, nc.vector.tensor_copy)
+        kv.append(second_factor(1))
+        bent0 = first_factor(0)
+        ka0 = weigh_first(0, bent0)
+        bent1 = first_factor(1)
+        ka1 = weigh_first(1, bent1)
+        bent2 = first_factor(2)
+        bent3 = first_factor(3)
+        update(0, ka0)
+        finish(0, 1)
+        ka2 = weigh_first(2, bent2)
+        update(1, ka1)
+        ka3 = weigh_first(3, bent3)
+        update(2, ka2)
+        finish(1, 2)
+        update(3, ka3)
+        finish(3, 1)

@@ -63,7 +63,7 @@ def tile_picked_yshamp_leak_p_kernel(
             )
 
         def load_py(h, o):
-            py_raw[h, o] = late.tile([P, PACK, HALF], F32, name="py_raw%d%d" % (h, o))
+            py_raw[h, o] = late.tile([P, PACK, HALF], F32, name="py_raw%d%d" % (h, o), tag="raw%d%d" % (h, o))
             rows = py[o * K_PASS : (o + 1) * K_PASS, h * HALF : (h + 1) * HALF]
             nc.sync.dma_start(out=py_raw[h, o][:], in_=rows.rearrange("(p j) n -> p j n", j=PACK))
 
@@ -94,14 +94,14 @@ def tile_picked_yshamp_leak_p_kernel(
         load_py(1, 1)
         nc.sync.dma_start(out=mom_sb[:], in_=mom.rearrange("(c p) m -> p c m", p=P))
 
-        def gather(dtype, table, b, name):
-            picked = keep.tile([P, K_PASS], dtype, name=name, align_bytes=64)
+        def gather(dtype, table, first, count, name):
+            picked = keep.tile([P, count * K_PASS], dtype, name=name, align_bytes=64)
             cols = K_PASS // 16
             nc.vector.tensor_copy(
-                out=picked[:].rearrange("p (j g r) -> p g j r", j=PACK, r=RUN),
-                in_=table.indirect(offsets[:, b * cols : (b + 1) * cols]),
+                out=picked[:].rearrange("p (b j g r) -> p b g j r", b=count, j=PACK, r=RUN),
+                in_=table.indirect(offsets[:, first * cols : (first + count) * cols]),
             )
-            return picked
+            return [picked[:, e * K_PASS : (e + 1) * K_PASS] for e in range(count)]
 
         def interleave(copy, dst, src):
             copy(
@@ -118,11 +118,15 @@ def tile_picked_yshamp_leak_p_kernel(
         x_code = {}
         x_scale = {}
 
-        def pick_words(o, b):
-            x_code[o, b] = gather(U32, word_table[o][:], b, "x_code%d%d" % (o, b))
+        def pick_words(o, first, count):
+            picked = gather(U32, word_table[o][:], first, count, "x_code%d%d" % (o, first))
+            for e in range(count):
+                x_code[o, first + e] = picked[e]
 
-        def pick_scales(b):
-            x_scale[b] = gather(U8, scale_table[:], b, "x_scale%d" % b)
+        def pick_scales():
+            picked = gather(U8, scale_table[:], 0, S_PASSES, "x_scale")
+            for b in range(S_PASSES):
+                x_scale[b] = picked[b]
 
         def prepare_pz():
             pz_bf = keep.tile([P, K_PASSES, N, PACK], BF16, name="pz_bf", align_bytes=64)
@@ -142,18 +146,18 @@ def tile_picked_yshamp_leak_p_kernel(
                 acc = one_pool.tile([P, PACK, COLS], F32, name="last_acc", tag="shared_bank")
             else:
                 acc = acc_pool.tile([P, PACK, COLS], F32, name="acc")
-            for j in range(PACK):
-                cols = slice(j * P, (j + 1) * P)
-                for o in range(K_PASSES):
-                    codes, scales = weights[o]
+            for o in range(K_PASSES):
+                codes, scales = weights[o]
+                for j in range(PACK):
+                    cols = slice(j * P, (j + 1) * P)
                     nc.tensor.matmul_mx(
                         out=acc[:, j, :],
                         lhsT=x_code[o, b][:, cols].bitcast(FP8X4),
                         lhsT_scale=x_scale[b][4 * o :, cols],
                         rhs=codes.bitcast(FP8X4),
                         rhs_scale=scales,
-                        start=(o == 0),
-                        stop=(o == K_PASSES - 1),
+                        start=(o == 0 and j == 0),
+                        stop=(o == K_PASSES - 1 and j == PACK - 1),
                     )
             return acc
 
@@ -166,7 +170,7 @@ def tile_picked_yshamp_leak_p_kernel(
 
         def second_factor(b):
             z = project(b, [(pz_q[0][:, o * N : (o + 1) * N], pz_q[1][:, o * N : (o + 1) * N]) for o in range(K_PASSES)])
-            sign = ring.tile([P, COLS, PACK], F32, name="sign")
+            sign = late.tile([P, COLS, PACK], F32, name="sign%d" % b, tag="sign" if b else "raw01")
             nc.scalar.activation(out=sign[:], in_=z[:].rearrange("p j n -> p n j"), func=ACT.Sign)
             scaled = ring.tile([P, PACK, COLS], F32, name="scaled")
             for j in range(PACK):
@@ -243,14 +247,12 @@ def tile_picked_yshamp_leak_p_kernel(
                 )
             nc.sync.dma_start(out=out_rows[:, cols, :], in_=result[:])
 
-        pick_scales(0)
-        pick_scales(1)
+        pick_scales()
         pz_q = prepare_pz()
-        pick_words(0, 0)
-        pick_words(0, 1)
+        pick_words(0, 0, S_PASSES)
         prepare_py(0, 0, nc.scalar.copy)
-        pick_words(1, 0)
-        pick_words(1, 1)
+        pick_words(1, 0, 1)
+        pick_words(1, 1, 1)
         prepare_py(0, 1, nc.scalar.copy)
         prepare_py(1, 0, nc.vector.tensor_copy)
         kv = [second_factor(0)]

from contextlib import ExitStack

import concourse.mybir as mybir

K, T, S, N, H = 1024, 2048, 1024, 128, 512
FLOPS = 2 * K * S * (H + N) + 2 * S * H * N

F32 = mybir.dt.float32
BF16 = mybir.dt.bfloat16
I32 = mybir.dt.int32
U32 = mybir.dt.uint32
U16 = mybir.dt.uint16
U8 = mybir.dt.uint8
FP8X4 = mybir.dt.float8_e4m3fn_x4
ACT = mybir.ActivationFunctionType
ALU = mybir.AluOpType

P = 128
PACK = 4
K_PASS = P * PACK
K_PASSES = K // K_PASS
S_PASSES = S // K_PASS
RUN = 8
HALF = 256
COLS = 128
CHUNKS = H // COLS


def tile_picked_yshamp_leak_p_kernel(
    tc, x_words, x_scales, py, pzz1, wa, wb, mom, offs, out
):
    nc = tc.nc
    with ExitStack() as ctx:
        keep = ctx.enter_context(tc.tile_pool(name="keep", bufs=1))
        ring = ctx.enter_context(tc.tile_pool(name="ring", bufs=4))
        acc_pool = ctx.enter_context(tc.psum_pool(name="acc", bufs=5))
        one_pool = ctx.enter_context(tc.psum_pool(name="one", bufs=1))

        offsets = keep.tile([P, S // 16], U16, name="offsets")
        nc.sync.dma_start(offsets[:], offs)
        scale_table = keep.tile([P, T], U8, name="scale_table", align_bytes=64)
        nc.vector.memset(scale_table[:].bitcast(I32), 0)
        factor_rows = keep.tile([P, S_PASSES * P], F32, name="factor_rows")
        nc.vector.memset(factor_rows[:], 0.0)
        identity = keep.tile([P, P], F32, name="identity")
        with tc.tile_pool(name="scratch", bufs=1) as scratch:
            zeros = scratch.tile([P, P], F32, name="zeros")
            nc.gpsimd.memset(zeros[:], 0.0)
            nc.gpsimd.affine_select(
                out=identity[:], in_=zeros[:], pattern=[[-1, P]], compare_op=ALU.not_equal, fill=1.0,
                base=0, channel_multiplier=1,
            )
        late = ctx.enter_context(tc.tile_pool(name="late", bufs=1))

        word_table = {}
        py_raw = {}

        def load_words(o):
            word_table[o] = late.tile([P, T], U32, name="word_table%d" % o, align_bytes=64)
            nc.sync.dma_start(
                out=word_table[o][:].bitcast(I32),
                in_=x_words[o].rearrange("p n t -> p (n t)").bitcast(I32),
            )

        def load_py(h, o):
            py_raw[h, o] = late.tile([P, PACK, HALF], F32, name="py_raw%d%d" % (h, o), tag="raw%d%d" % (h, o))
            rows = py[o * K_PASS : (o + 1) * K_PASS, h * HALF : (h + 1) * HALF]
            nc.sync.dma_start(out=py_raw[h, o][:], in_=rows.rearrange("(p j) n -> p j n", j=PACK))

        def load_scales():
            for q in range(4):
                nc.sync.dma_start(
                    out=scale_table[32 * q : 32 * q + 4 * K_PASSES, :].bitcast(I32),
                    in_=x_scales[:, 4 * q : 4 * q + 4, :].bitcast(I32),
                )

        def load_factors():
            for a, w in enumerate((wa, wb)):
                nc.sync.dma_start(
                    out=factor_rows[PACK * a : PACK * (a + 1), :].rearrange("j (g r) -> j g r", r=RUN),
                    in_=w.rearrange("(g j r) o -> j g (r o)", j=PACK, r=RUN),
                )

        pz_raw = keep.tile([P, K_PASSES, PACK, N], F32, name="pz_raw")
        mom_sb = late.tile([P, CHUNKS, N], F32, name="mom_sb")
        nc.sync.dma_start(out=pz_raw[:], in_=pzz1.rearrange("(o p j) n -> p o j n", o=K_PASSES, j=PACK))
        load_scales()
        load_factors()
        load_words(0)
        load_py(0, 0)
        load_words(1)
        load_py(0, 1)
        load_py(1, 0)
        load_py(1, 1)
        nc.sync.dma_start(out=mom_sb[:], in_=mom.rearrange("(c p) m -> p c m", p=P))

        def gather(dtype, table, first, count, name):
            picked = keep.tile([P, count * K_PASS], dtype, name=name, align_bytes=64)
            cols = K_PASS // 16
            nc.vector.tensor_copy(
                out=picked[:].rearrange("p (b j g r) -> p b g j r", b=count, j=PACK, r=RUN),
                in_=table.indirect(offsets[:, first * cols : (first + count) * cols]),
            )
            return [picked[:, e * K_PASS : (e + 1) * K_PASS] for e in range(count)]

        def interleave(copy, dst, src):
            copy(
                out=dst.rearrange("p (c i) t -> p c t i", i=4),
                in_=src.rearrange("p t (c i) -> p c t i", i=4),
            )

        def quantise(values, width, name):
            codes = keep.tile([P, width], U32, name=name + "_codes", align_bytes=64)
            scales = keep.tile([P, width], U8, name=name + "_scales", align_bytes=64)
            nc.vector.quantize_mx(out=codes[:].bitcast(FP8X4), scales=scales[:], in_=values)
            return codes, scales

        x_code = {}
        x_scale = {}

        def pick_words(o, first, count):
            picked = gather(U32, word_table[o][:], first, count, "x_code%d%d" % (o, first))
            for e in range(count):
                x_code[o, first + e] = picked[e]

        def pick_scales():
            picked = gather(U8, scale_table[:], 0, S_PASSES, "x_scale")
            for b in range(S_PASSES):
                x_scale[b] = picked[b]

        def prepare_pz():
            pz_bf = keep.tile([P, K_PASSES, N, PACK], BF16, name="pz_bf", align_bytes=64)
            for o in range(K_PASSES):
                interleave(nc.scalar.copy, pz_bf[:, o], pz_raw[:, o])
            return quantise(pz_bf[:].rearrange("p o n t -> p (o n t)"), K_PASSES * N, "pz")

        turned = one_pool.tile([P, S_PASSES, P], F32, name="turned", tag="shared_bank")
        for b in range(S_PASSES):
            nc.tensor.transpose(turned[:, b, :], factor_rows[:, b * P : (b + 1) * P], identity[:])
        factors = keep.tile([P, S_PASSES, 2 * PACK], F32, name="factors")
        nc.scalar.activation(out=factors[:, :, 0:PACK], in_=turned[:, :, 0:PACK], func=ACT.Copy)
        nc.scalar.activation(out=factors[:, :, PACK:], in_=turned[:, :, PACK : 2 * PACK], func=ACT.Copy, scale=-0.25)

        def project(b, weights, last=False):
            if last:
                acc = one_pool.tile([P, PACK, COLS], F32, name="last_acc", tag="shared_bank")
            else:
                acc = acc_pool.tile([P, PACK, COLS], F32, name="acc")
            for o in range(K_PASSES):
                codes, scales = weights[o]
                for j in range(PACK):
                    cols = slice(j * P, (j + 1) * P)
                    nc.tensor.matmul_mx(
                        out=acc[:, j, :],
                        lhsT=x_code[o, b][:, cols].bitcast(FP8X4),
                        lhsT_scale=x_scale[b][4 * o :, cols],
                        rhs=codes.bitcast(FP8X4),
                        rhs_scale=scales,
                        start=(o == 0 and j == 0),
                        stop=(o == K_PASSES - 1 and j == PACK - 1),
                    )
            return acc

        py_q = {}

        def prepare_py(h, o, copy):
            py_bf = ring.tile([P, HALF, PACK], BF16, name="py_bf", align_bytes=64)
            interleave(copy, py_bf[:], py_raw[h, o][:])
            py_q[h, o] = quantise(py_bf[:].rearrange("p n t -> p (n t)"), HALF, "py%d%d" % (h, o))

        def second_factor(b):
            z = project(b, [(pz_q[0][:, o * N : (o + 1) * N], pz_q[1][:, o * N : (o + 1) * N]) for o in range(K_PASSES)])
            sign = late.tile([P, COLS, PACK], F32, name="sign%d" % b, tag="sign" if b else "raw01")
            nc.scalar.activation(out=sign[:], in_=z[:].rearrange("p j n -> p n j"), func=ACT.Sign)
            scaled = ring.tile([P, PACK, COLS], F32, name="scaled")
            for j in range(PACK):
                nc.scalar.activation(
                    out=scaled[:, j, :], in_=z[:, j, :], func=ACT.Copy, scale=factors[:, b, PACK + j : PACK + j + 1]
                )
            rounded = ring.tile([P, COLS, PACK], BF16, name="kv_rounded", align_bytes=64)
            nc.vector.scalar_tensor_tensor(
                out=rounded[:], in0=sign[:], scalar=-3.0, in1=scaled[:].rearrange("p j n -> p n j"),
                op0=ALU.add, op1=ALU.mult,
            )
            return quantise(rounded[:].rearrange("p n j -> p (n j)"), COLS, "kv%d" % b)

        def first_factor(c):
            h, lo = divmod(c * COLS, HALF)
            cols = slice(lo, lo + COLS)
            bent = ring.tile([P, S_PASSES, COLS, PACK], F32, name="bent")
            for b in range(S_PASSES):
                weights = [(py_q[h, o][0][:, cols], py_q[h, o][1][:, cols]) for o in range(K_PASSES)]
                y = project(b, weights, last=(c == CHUNKS - 1 and b == S_PASSES - 1))
                nc.scalar.activation(out=bent[:, b], in_=y[:].rearrange("p j n -> p n j"), func=ACT.Tanh)
            return bent

        def weigh_first(c, bent):
            rounded = ring.tile([P, S_PASSES, COLS, PACK], BF16, name="ka_rounded", align_bytes=64)
            factor = factors[:, :, 0:PACK].unsqueeze(2).to_broadcast([P, S_PASSES, COLS, PACK])
            nc.vector.tensor_tensor(out=rounded[:], in0=bent[:], in1=factor, op=ALU.mult)
            return quantise(rounded[:].rearrange("p b n j -> p (b n j)"), S_PASSES * COLS, "ka%d" % c)

        moment = keep.tile([P, CHUNKS, N], F32, name="moment")
        first_sum = keep.tile([P, 1], F32, name="first_sum", tag="sum_then_squares")
        later_sums = keep.tile([P, CHUNKS - 1], F32, name="later_sums")

        def update(c, ka):
            outer = one_pool.tile([P, N], F32, name="outer%d" % c, tag="outer%d" % (c % 2) if c else "shared_bank")
            for b in range(S_PASSES):
                cols = slice(b * COLS, (b + 1) * COLS)
                nc.tensor.matmul_mx(
                    out=outer[:],
                    lhsT=ka[0][:, cols].bitcast(FP8X4),
                    lhsT_scale=ka[1][:, cols],
                    rhs=kv[b][0][:].bitcast(FP8X4),
                    rhs_scale=kv[b][1][:],
                    start=(b == 0),
                    stop=(b == S_PASSES - 1),
                )
            nc.vector.scalar_tensor_tensor(
                out=moment[:, c, :], in0=mom_sb[:, c, :], scalar=0.7, in1=outer[:], op0=ALU.mult, op1=ALU.add
            )
            if c == 0:
                squares = keep.tile([P, N], F32, name="first_squares")
                nc.vector.scalar_tensor_tensor(
                    out=squares[:], in0=moment[:, c, :], scalar=1.0 / N, in1=moment[:, c, :],
                    op0=ALU.mult, op1=ALU.mult, accum_out=first_sum[:],
                )
            else:
                squares = keep.tile([P, N], F32, name="squares%d" % c, tag="sum_then_squares")
                nc.scalar.activation(
                    out=squares[:], in_=moment[:, c, :], func=ACT.Square, scale=N**-0.5,
                    accum_out=later_sums[:, c - 1 : c],
                )

        out_rows = out.rearrange("(c p) m -> p c m", p=P)

        def finish(first, count):
            cols = slice(first, first + count)
            means = later_sums[:, first - 1 : first - 1 + count] if first else first_sum[:]
            inv_rms = keep.tile([P, count], F32, name="inv_rms%d" % first)
            nc.scalar.activation(out=inv_rms[:], in_=means, func=ACT.Abs_reciprocal_sqrt, bias=0.1)
            result = keep.tile([P, count, N], F32, name="result%d" % first)
            for e in range(count):
                nc.scalar.activation(
                    out=result[:, e, :], in_=moment[:, first + e, :], func=ACT.Copy, scale=inv_rms[:, e : e + 1]
                )
            nc.sync.dma_start(out=out_rows[:, cols, :], in_=result[:])

        pick_scales()
        pz_q = prepare_pz()
        pick_words(0, 0, S_PASSES)
        prepare_py(0, 0, nc.scalar.copy)
        pick_words(1, 0, 1)
        pick_words(1, 1, 1)
        prepare_py(0, 1, nc.scalar.copy)
        prepare_py(1, 0, nc.vector.tensor_copy)
        kv = [second_factor(0)]
        prepare_py(1, 1, nc.vector.tensor_copy)
        kv.append(second_factor(1))
        bent0 = first_factor(0)
        ka0 = weigh_first(0, bent0)
        bent1 = first_factor(1)
        ka1 = weigh_first(1, bent1)
        bent2 = first_factor(2)
        bent3 = first_factor(3)
        update(0, ka0)
        finish(0, 1)
        ka2 = weigh_first(2, bent2)
        update(1, ka1)
        ka3 = weigh_first(3, bent3)
        update(2, ka2)
        finish(1, 2)
        update(3, ka3)
        finish(3, 1)
